import numpy as np
import ml_dtypes


def mxq(x, axis, fmt="e4m3"):
    dtype, down = {"e4m3": (ml_dtypes.float8_e4m3fn, 7), "e5m2": (ml_dtypes.float8_e5m2, 14)}[fmt]
    v = np.moveaxis(np.asarray(x, np.float32).astype(ml_dtypes.bfloat16).astype(np.float64), axis, -1)
    blocks = v.reshape(v.shape[:-1] + (-1, 32))
    amax = np.abs(blocks).max(-1, keepdims=True)
    byte = np.maximum(np.where(amax > 0, np.frexp(amax)[1] - 1 + 127, 0) - down, 1)
    scale = np.exp2(byte - 127.0)
    codes = (blocks / scale).astype(np.float32).astype(dtype).astype(np.float64)
    return np.moveaxis((codes * scale).reshape(v.shape), -1, axis)


WIDE = False


def mx_kscale(k):
    if not WIDE:
        return np.ones(k)
    levels = np.array([10, -10, 5, -5, 0])
    if k % 512:
        return np.exp2(np.random.permutation(np.resize(levels, k // 32))).repeat(32)
    a = np.empty((k // 512, 16))
    for p in range(k // 512):
        a[p, :8] = np.random.permutation(np.resize(levels, 8))
        for g in range(8):
            far = levels[np.abs(levels - a[p, g]) >= 10]
            a[p, g + 8] = far[np.random.randint(len(far))]
    return np.exp2(a.ravel()).repeat(32)


def f64(x):
    return np.asarray(x).astype(np.float64)


def striped(idx):
    return np.tile(idx.reshape(-1, 16).T, (8, 1)).astype(np.uint16)


def unstriped(offs):
    return offs[:16].T.reshape(-1).astype(np.int64)


def striped8(idx):
    return np.concatenate([x.reshape(-1, 16).T for x in idx]).astype(np.uint16)


def runs(offs, k):
    lists = np.stack([offs[16 * r : 16 * r + 16].T.reshape(-1) for r in range(8)]).astype(np.int64)
    return lists[np.arange(k) % 512 // 64]


def pack_weight(w):
    k, n = w.shape
    w = f64(np.asarray(w, np.float32).astype(ml_dtypes.bfloat16)).reshape(k // 32, 32, n)
    amax = np.abs(w).max(1)
    byte = np.clip(np.where(amax > 0, np.frexp(amax)[1] - 1 + 127 - 7, 1), 1, 254)
    scaled = (w * np.exp2(127.0 - byte)[:, None, :]).reshape(k, n).astype(np.float32)
    words = np.ascontiguousarray(scaled.reshape(k // 512, 128, 4, n).transpose(0, 1, 3, 2)).astype(ml_dtypes.float8_e4m3fn).view(np.uint8)
    return words, np.ascontiguousarray(byte.astype(np.uint8).reshape(k // 512, 16, n))


def unpack_weight(words, scales):
    g, p, n, _ = words.shape
    vals = np.ascontiguousarray(words).view(ml_dtypes.float8_e4m3fn).astype(np.float64) * np.repeat(np.exp2(scales.astype(np.float64) - 127.0), 8, axis=1)[..., None]
    return vals.transpose(0, 1, 3, 2).reshape(g * 512, n)

def planes(y):
    n, m = y.shape
    v = y.astype(np.float32).astype(ml_dtypes.bfloat16).astype(np.float64).reshape(n // 32, 32, m)
    top = np.abs(v).max(1)
    byte = np.clip(np.where(top > 0, np.frexp(top)[1] - 1 + 127 - 7, 1), 1, 254)
    codes = (v * np.exp2(127.0 - byte)[:, None, :]).reshape(n, m).astype(np.float32).astype(ml_dtypes.float8_e4m3fn).view(np.uint8)
    words = codes.reshape(n // 512, 128, 4, m).transpose(0, 1, 3, 2)
    return np.ascontiguousarray(words), np.ascontiguousarray(byte.astype(np.uint8).reshape(n // 512, 16, m))


K, T, S, H = 512, 2048, 512, 512


def setup_inputs():
    n = np.random.standard_normal
    s = mx_kscale(K)[:, None]
    u = mx_kscale(S)
    packed_xT = pack_weight(n((K, T)) * s)
    packed_w1 = pack_weight(n((K, H)) / np.sqrt(K) / s)
    return {
        "x_words": packed_xT[0],
        "x_scales": packed_xT[1],
        "w1_words": packed_w1[0],
        "w1_scales": packed_w1[1],
        "ga": (np.random.uniform(0.5, 1.5, (H, 1)) * u[:, None]).astype(np.float32),
        "gb": (np.random.uniform(0.5, 1.5, (H, 1)) / u[:, None]).astype(np.float32),
        "offs": striped(np.random.permutation(T)[:S]),
        "n1": striped8(np.stack([np.random.permutation(S) for _ in range(8)])),
        "n2": striped8(np.stack([np.random.permutation(S) for _ in range(8)])),
        "n3": striped8(np.stack([np.random.permutation(S) for _ in range(8)])),
        "n4": striped8(np.stack([np.random.permutation(S) for _ in range(8)])),
        "n5": striped8(np.stack([np.random.permutation(S) for _ in range(8)])),
        "n6": striped8(np.stack([np.random.permutation(S) for _ in range(8)])),
        "n7": striped8(np.stack([np.random.permutation(S) for _ in range(8)])),
    }


def reference(x_words, x_scales, w1_words, w1_scales, ga, gb, offs, n1, n2, n3, n4, n5, n6, n7):
    xq = unpack_weight(x_words, x_scales)[:, unstriped(offs)]
    y = unpack_weight(w1_words, w1_scales).T @ xq
    z = f64(ga) * (0.75 * (y * (y[np.arange(H)[:, None], runs(n1, H)]) + (y[np.arange(H)[:, None], runs(n2, H)]) * (y[np.arange(H)[:, None], runs(n3, H)])))
    z2 = f64(gb) * ((y[np.arange(H)[:, None], runs(n4, H)]) * (y[np.arange(H)[:, None], runs(n5, H)]))
    s = 0.0625 * ((mxq(z, 0, "e4m3").T @ mxq(z2, 0, "e4m3")))
    st = s - (s[np.arange(S)[:, None], runs(n6, S)])
    out_0 = np.maximum(st, st[np.arange(S)[:, None], runs(n7, S)])
    return (out_0,) + planes(out_0)

@@ -1,0 +1,230 @@
+from contextlib import ExitStack
+
+import concourse.mybir as mybir
+from concourse.masks import make_identity
+
+F32 = mybir.dt.float32
+BF16 = mybir.dt.bfloat16
+I32 = mybir.dt.int32
+U32 = mybir.dt.uint32
+U16 = mybir.dt.uint16
+U8 = mybir.dt.uint8
+FP8X4 = mybir.dt.float8_e4m3fn_x4
+MULT = mybir.AluOpType.mult
+SUB = mybir.AluOpType.subtract
+MAX = mybir.AluOpType.max
+COPY = mybir.ActivationFunctionType.Copy
+
+P = 128
+PACK = 4
+T = 2048
+S = 512
+WIDE = 2 * S
+FLOPS = 2 * 2 * 512 * 512 * 512
+
+
+def entries(offsets, lo, hi):
+    return offsets[:, lo // 16 : hi // 16]
+
+
+def tile_picked_selfdotprodhopmx_none_po_kernel(
+    tc, x_words, x_scales, w1_words, w1_scales, ga, gb, offs, n1, n2, n3, n4, n5, n6, n7, out_0, out_1, out_2
+):
+    nc = tc.nc
+    with ExitStack() as ctx:
+        keep = ctx.enter_context(tc.tile_pool(name="keep", bufs=1))
+        psum = ctx.enter_context(tc.psum_pool(name="psum", bufs=1))
+
+        def sb(name, shape, dtype):
+            return keep.tile(shape, dtype, name=name, align_bytes=64)
+
+        banks = [psum.tile([P, S], F32, name="bank%d" % b) for b in range(8)]
+
+        def load_list(name, src):
+            tile = keep.tile([P, S // 16], U16, name=name)
+            nc.sync.dma_start(tile[:], src)
+            return tile
+
+        def load_scales(tile, src, queue):
+            for q in range(4):
+                queue.dma_start(tile[32 * q : 32 * q + 4, :].bitcast(I32), src[0, 4 * q : 4 * q + 4, :].bitcast(I32))
+
+        xs = sb("xs", [P, T], U8)
+        ws = sb("ws", [P, S], U8)
+        nc.vector.memset(xs[:].bitcast(I32), 0)
+        nc.vector.memset(ws[:].bitcast(I32), 0)
+        load_scales(xs, x_scales, nc.scalar)
+        picks = load_list("picks", offs)
+        xw = sb("xw", [P, T], I32)
+        nc.sync.dma_start(xw[:], x_words[0].rearrange("p n t -> p (n t)").bitcast(I32))
+        ww = sb("ww", [P, S], I32)
+        nc.sync.dma_start(ww[:], w1_words[0].rearrange("p n t -> p (n t)").bitcast(I32))
+        ga_t = sb("ga_t", [P, PACK], F32)
+        nc.sync.dma_start(ga_t[:], ga.rearrange("(p t) o -> p (t o)", t=PACK))
+        load_scales(ws, w1_scales, nc.scalar)
+        l2 = load_list("l2", n2)
+        l1 = load_list("l1", n1)
+        l3 = load_list("l3", n3)
+        gb_t = sb("gb_t", [P, PACK], F32)
+        nc.sync.dma_start(gb_t[:], gb.rearrange("(p t) o -> p (t o)", t=PACK))
+        l4 = load_list("l4", n4)
+        l5 = load_list("l5", n5)
+        l6 = load_list("l6", n6)
+        l7 = load_list("l7", n7)
+
+        ident = sb("ident", [P, P], F32)
+        make_identity(nc, ident[:])
+        ca = sb("ca", [P, PACK], F32)
+        nc.scalar.activation(ca[:], ga_t[:], COPY, scale=0.75)
+
+        y = [sb("y%d" % t, [P, WIDE], F32) for t in range(PACK)]
+        ya = [sb("ya%d" % t, [P, WIDE], F32) for t in range(PACK)]
+        yb = [sb("yb%d" % t, [P, S], F32) for t in range(PACK)]
+        for t in range(PACK):
+            nc.vector.memset(ya[t][:, S:], 0.0)
+            nc.vector.memset(y[t][:, S:], 0.0)
+
+        xgs = sb("xgs", [P, S], U8)
+        nc.vector.tensor_copy(xgs[:], xs[:].indirect(picks[:]))
+        wd = sb("wd", [P, S], I32)
+        wds = sb("wds", [P, S], U8)
+        nc.vector.tensor_copy(wd[:].rearrange("p (t m) -> p t m", t=PACK), ww[:].rearrange("p (m t) -> p t m", t=PACK))
+        nc.vector.tensor_copy(wds[:].rearrange("p (t m) -> p t m", t=PACK), ws[:].rearrange("p (m t) -> p t m", t=PACK))
+        xg = sb("xg", [P, S], U32)
+        half = S // 2
+
+        def mx(out, codes_l, scales_l, codes_r, scales_r):
+            nc.tensor.matmul_mx(out, lhsT=codes_l.bitcast(FP8X4), lhsT_scale=scales_l, rhs=codes_r.bitcast(FP8X4),
+                                rhs_scale=scales_r, start=True, stop=True)
+
+        first_banks = [banks[0], banks[4]]
+        for h in range(2):
+            cols = slice(h * half, (h + 1) * half)
+            nc.vector.tensor_copy(xg[:, cols], xw[:].bitcast(U32).indirect(entries(picks, h * half, (h + 1) * half)))
+            mx(first_banks[h][:, :half], wd[:, :P], wds[:, :P], xg[:, cols], xgs[:, cols])
+            nc.scalar.activation(ya[0][:, cols], first_banks[h][:, :half], COPY, scale=ca[:, 0:1])
+            nc.scalar.copy(y[0][:, cols], first_banks[h][:, :half])
+        for t in range(1, PACK):
+            rows = slice(t * P, (t + 1) * P)
+            mx(banks[t][:], wd[:, rows], wds[:, rows], xg[:], xgs[:])
+            nc.scalar.activation(ya[t][:, :S], banks[t][:], COPY, scale=ca[:, t : t + 1])
+            nc.scalar.copy(y[t][:, :S], banks[t][:])
+        for h in range(2):
+            cols = slice(h * half, (h + 1) * half)
+            nc.scalar.activation(yb[0][:, cols], first_banks[h][:, :half], COPY, scale=gb_t[:, 0:1])
+        for t in range(1, PACK):
+            nc.scalar.activation(yb[t][:], banks[t][:], COPY, scale=gb_t[:, t : t + 1])
+
+        for t in range(PACK):
+            g2 = sb("g2_%d" % t, [P, S], F32)
+            prod1 = sb("prod1_%d" % t, [P, S], F32)
+            prod23 = sb("prod23_%d" % t, [P, S], F32)
+            nc.vector.tensor_copy(g2[:], ya[t][:].indirect(l2[:]))
+            nc.vector.tensor_tensor(prod1[:], y[t][:].indirect(l1[:]), ya[t][:, :S], MULT)
+            nc.vector.tensor_tensor(prod23[:], y[t][:].indirect(l3[:]), g2[:], MULT)
+            for b in range(4):
+                dst = banks[4 + b][:, t * P : (t + 1) * P]
+                cols = slice(b * P, (b + 1) * P)
+                nc.tensor.matmul(dst, prod1[:, cols], ident[:], start=True, stop=False, is_transpose=True)
+                nc.tensor.matmul(dst, prod23[:, cols], ident[:], start=False, stop=True, is_transpose=True)
+        z_in = sb("z_in", [P, PACK * S], BF16)
+        z_pairs = z_in[:].bitcast(F32).rearrange("p (t m u) -> p t m u", t=PACK, u=2)
+        for h in range(2):
+            for bb in range(2):
+                b = 2 * h + bb
+                zt = sb("zt%d" % b, [P, S], BF16)
+                nc.scalar.copy(zt[:].rearrange("q (u p e) -> q u p e", u=2, e=2),
+                               banks[4 + b][:].rearrange("q (u e p) -> q u p e", u=2, e=2))
+                for u in range(2):
+                    nc.tensor.transpose(banks[h][:, u * half + bb * P : u * half + (bb + 1) * P],
+                                        zt[:].bitcast(F32)[:, u * P : (u + 1) * P], ident[:])
+            nc.scalar.copy(z_pairs[:, :, 64 * h : 64 * (h + 1), :], banks[h][:].rearrange("p (u m t) -> p t m u", u=2, t=PACK))
+        zq = sb("zq", [P, S], U32)
+        zs = sb("zs", [P, S], U8)
+
+        v = [sb("v%d" % t, [P, S], F32) for t in range(PACK)]
+        stretches = [(0, 256), (256, 384), (384, 512)]
+
+        def z2_lookups(c):
+            lo, hi = stretches[c]
+            g4 = sb("g4_%d" % c, [P, PACK, hi - lo], F32)
+            z2 = sb("z2_%d" % c, [P, PACK, hi - lo], F32)
+            for t in range(PACK):
+                nc.vector.tensor_copy(g4[:, t, :], yb[t][:].indirect(entries(l4, lo, hi)))
+            for t in range(PACK):
+                nc.vector.tensor_tensor(z2[:, t, :], y[t][:].indirect(entries(l5, lo, hi)), g4[:, t, :], MULT)
+            return z2
+
+        def interleave(name, src, copy):
+            width = src.shape[2]
+            dst = sb(name, [P, PACK * width], BF16)
+            copy(dst[:].rearrange("p (c t) -> p c t", t=PACK), src.rearrange("p t c -> p c t"))
+            return dst
+
+        def s_columns(c, z2_in):
+            lo, hi = stretches[c]
+            codes = sb("z2q%d" % c, [P, hi - lo], U32)
+            scales = sb("z2s%d" % c, [P, hi - lo], U8)
+            nc.vector.quantize_mx(codes[:].bitcast(FP8X4), scales[:], z2_in[:])
+            for t in range(PACK):
+                rows = slice(t * P, (t + 1) * P)
+                if c == 0:
+                    dst = banks[2 + t // 2][:, (t % 2) * half : (t % 2 + 1) * half]
+                else:
+                    dst = banks[4 + t][:, lo - half : hi - half]
+                mx(dst, zq[:, rows], zs[:, rows], codes[:], scales[:])
+
+        def s_out(t, h):
+            cols = slice(h * half, (h + 1) * half)
+            src = banks[2 + t // 2][:, (t % 2) * half : (t % 2 + 1) * half] if h == 0 else banks[4 + t][:, :half]
+            nc.scalar.activation(ya[t][:, cols], src, COPY, scale=-0.0625)
+            nc.scalar.activation(v[t][:, cols], src, COPY, scale=-0.0625)
+
+        z2_0 = z2_lookups(0)
+        nc.vector.quantize_mx(zq[:].bitcast(FP8X4), zs[:], z_in[:])
+        in_0 = interleave("z2in0", z2_0[:], nc.scalar.copy)
+        z2_1 = z2_lookups(1)
+        s_columns(0, in_0)
+        in_1 = interleave("z2in1", z2_1[:], nc.scalar.copy)
+        for t in range(PACK):
+            s_out(t, 0)
+        z2_2 = z2_lookups(2)
+        in_2 = interleave("z2in2", z2_2[:], nc.vector.tensor_copy)
+        s_columns(1, in_1)
+        s_columns(2, in_2)
+        for t in range(PACK):
+            s_out(t, 1)
+
+        st = [sb("st%d" % t, [P, S], F32) for t in range(PACK)]
+        for t in range(PACK):
+            nc.vector.tensor_tensor(st[t][:], ya[t][:].indirect(l6[:]), v[t][:], SUB)
+        out_rows = out_0.rearrange("(p t) j -> p t j", t=PACK)
+        out_words = out_1[0].rearrange("p n t -> p (n t)").bitcast(I32)
+        oq = sb("oq", [P, S], U32)
+        osc = sb("osc", [P, S], U8)
+
+        def out_lookups(name, lo, hi):
+            g7 = sb("g7_" + name, [P, PACK, hi - lo], F32)
+            res = sb("res_" + name, [P, PACK, hi - lo], F32)
+            for t in range(PACK):
+                nc.vector.tensor_copy(g7[:, t, :], st[t][:].indirect(entries(l7, lo, hi)))
+            for t in range(PACK):
+                nc.vector.tensor_tensor(res[:, t, :], g7[:, t, :], st[t][:, lo:hi], MAX)
+            nc.sync.dma_start(out_rows[:, :, lo:hi], res[:])
+            return res
+
+        def out_planes(lo, hi, rounded):
+            nc.vector.quantize_mx(oq[:, lo:hi].bitcast(FP8X4), osc[:, lo:hi], rounded[:])
+            nc.sync.dma_start(out_words[:, lo:hi], oq[:, lo:hi].bitcast(I32))
+
+        res_a = out_lookups("a", 0, 384)
+        r0 = interleave("r0", res_a[:, :, 0:256], nc.scalar.copy)
+        r1 = interleave("r1", res_a[:, :, 256:384], nc.scalar.copy)
+        res_b = out_lookups("b", 384, 512)
+        out_planes(0, 256, r0)
+        r2 = interleave("r2", res_b[:], nc.vector.tensor_copy)
+        out_planes(256, 384, r1)
+        out_planes(384, 512, r2)
+        for q in range(4):
+            queue = nc.scalar if q % 2 == 0 else nc.sync
+            queue.dma_start(out_2[0, 4 * q : 4 * q + 4, :].bitcast(I32), osc[32 * q : 32 * q + 4, :].bitcast(I32))

@@ -35,8 +35,8 @@ def tile_picked_selfdotprodhopmx_none_po_kernel(
         keep = ctx.enter_context(tc.tile_pool(name="keep", bufs=1))
         psum = ctx.enter_context(tc.psum_pool(name="psum", bufs=1))
 
-        def sb(name, shape, dtype):
-            return keep.tile(shape, dtype, name=name, align_bytes=64)
+        def sb(name, shape, dtype, tag=None):
+            return keep.tile(shape, dtype, name=name, tag=tag or name, align_bytes=64)
 
         banks = [psum.tile([P, S], F32, name="bank%d" % b) for b in range(8)]
 
@@ -47,21 +47,19 @@ def tile_picked_selfdotprodhopmx_none_po_kernel(
 
         def load_scales(tile, src, queue):
             for q in range(4):
-                queue.dma_start(tile[32 * q : 32 * q + 4, :].bitcast(I32), src[0, 4 * q : 4 * q + 4, :].bitcast(I32))
+                queue.dma_start(tile[32 * q : 32 * (q + 1), :].bitcast(I32), src[0, 4 * q : 4 * q + 4, :].bitcast(I32).partition_broadcast(8))
 
         xs = sb("xs", [P, T], U8)
         ws = sb("ws", [P, S], U8)
-        nc.vector.memset(xs[:].bitcast(I32), 0)
-        nc.vector.memset(ws[:].bitcast(I32), 0)
-        load_scales(xs, x_scales, nc.scalar)
+        ga_t = sb("ga_t", [P, PACK], F32)
+        nc.scalar.dma_start(ga_t[:], ga.rearrange("(p t) o -> p (t o)", t=PACK))
+        load_scales(xs, x_scales, nc.sync)
         picks = load_list("picks", offs)
         xw = sb("xw", [P, T], I32)
         nc.sync.dma_start(xw[:], x_words[0].rearrange("p n t -> p (n t)").bitcast(I32))
+        load_scales(ws, w1_scales, nc.sync)
         ww = sb("ww", [P, S], I32)
         nc.sync.dma_start(ww[:], w1_words[0].rearrange("p n t -> p (n t)").bitcast(I32))
-        ga_t = sb("ga_t", [P, PACK], F32)
-        nc.sync.dma_start(ga_t[:], ga.rearrange("(p t) o -> p (t o)", t=PACK))
-        load_scales(ws, w1_scales, nc.scalar)
         l2 = load_list("l2", n2)
         l1 = load_list("l1", n1)
         l3 = load_list("l3", n3)
@@ -74,22 +72,23 @@ def tile_picked_selfdotprodhopmx_none_po_kernel(
 
         ident = sb("ident", [P, P], F32)
         make_identity(nc, ident[:])
-        ca = sb("ca", [P, PACK], F32)
-        nc.scalar.activation(ca[:], ga_t[:], COPY, scale=0.75)
 
         y = [sb("y%d" % t, [P, WIDE], F32) for t in range(PACK)]
         ya = [sb("ya%d" % t, [P, WIDE], F32) for t in range(PACK)]
         yb = [sb("yb%d" % t, [P, S], F32) for t in range(PACK)]
         for t in range(PACK):
-            nc.vector.memset(ya[t][:, S:], 0.0)
-            nc.vector.memset(y[t][:, S:], 0.0)
+            engine = nc.vector if t < 2 else nc.gpsimd
+            engine.memset(ya[t][:, S:], 0.0)
+            engine.memset(y[t][:, S:], 0.0)
 
         xgs = sb("xgs", [P, S], U8)
         nc.vector.tensor_copy(xgs[:], xs[:].indirect(picks[:]))
         wd = sb("wd", [P, S], I32)
         wds = sb("wds", [P, S], U8)
-        nc.vector.tensor_copy(wd[:].rearrange("p (t m) -> p t m", t=PACK), ww[:].rearrange("p (m t) -> p t m", t=PACK))
-        nc.vector.tensor_copy(wds[:].rearrange("p (t m) -> p t m", t=PACK), ws[:].rearrange("p (m t) -> p t m", t=PACK))
+        wd_to = wd[:].rearrange("p (t m) -> p t m", t=PACK)
+        wd_from = ww[:].rearrange("p (m t) -> p t m", t=PACK)
+        wds_to = wds[:].rearrange("p (t m) -> p t m", t=PACK)
+        wds_from = ws[:].rearrange("p (m t) -> p t m", t=PACK)
         xg = sb("xg", [P, S], U32)
         half = S // 2
 
@@ -101,13 +100,19 @@ def tile_picked_selfdotprodhopmx_none_po_kernel(
         for h in range(2):
             cols = slice(h * half, (h + 1) * half)
             nc.vector.tensor_copy(xg[:, cols], xw[:].bitcast(U32).indirect(entries(picks, h * half, (h + 1) * half)))
+            if h == 0:
+                nc.vector.tensor_copy(wds_to[:, 0, :], wds_from[:, 0, :])
+                nc.vector.tensor_copy(wd_to[:, 0, :], wd_from[:, 0, :])
+            else:
+                nc.vector.tensor_copy(wds_to[:, 1:, :], wds_from[:, 1:, :])
+                nc.vector.tensor_copy(wd_to[:, 1:, :], wd_from[:, 1:, :])
             mx(first_banks[h][:, :half], wd[:, :P], wds[:, :P], xg[:, cols], xgs[:, cols])
-            nc.scalar.activation(ya[0][:, cols], first_banks[h][:, :half], COPY, scale=ca[:, 0:1])
+            nc.scalar.activation(ya[0][:, cols], first_banks[h][:, :half], COPY, scale=ga_t[:, 0:1])
             nc.scalar.copy(y[0][:, cols], first_banks[h][:, :half])
         for t in range(1, PACK):
             rows = slice(t * P, (t + 1) * P)
             mx(banks[t][:], wd[:, rows], wds[:, rows], xg[:], xgs[:])
-            nc.scalar.activation(ya[t][:, :S], banks[t][:], COPY, scale=ca[:, t : t + 1])
+            nc.scalar.activation(ya[t][:, :S], banks[t][:], COPY, scale=ga_t[:, t : t + 1])
             nc.scalar.copy(y[t][:, :S], banks[t][:])
         for h in range(2):
             cols = slice(h * half, (h + 1) * half)
@@ -133,8 +138,8 @@ def tile_picked_selfdotprodhopmx_none_po_kernel(
             for bb in range(2):
                 b = 2 * h + bb
                 zt = sb("zt%d" % b, [P, S], BF16)
-                nc.scalar.copy(zt[:].rearrange("q (u p e) -> q u p e", u=2, e=2),
-                               banks[4 + b][:].rearrange("q (u e p) -> q u p e", u=2, e=2))
+                nc.scalar.activation(zt[:].rearrange("q (u p e) -> q u p e", u=2, e=2),
+                                     banks[4 + b][:].rearrange("q (u e p) -> q u p e", u=2, e=2), COPY, scale=0.75)
                 for u in range(2):
                     nc.tensor.transpose(banks[h][:, u * half + bb * P : u * half + (bb + 1) * P],
                                         zt[:].bitcast(F32)[:, u * P : (u + 1) * P], ident[:])
@@ -147,10 +152,12 @@ def tile_picked_selfdotprodhopmx_none_po_kernel(
 
         def z2_lookups(c):
             lo, hi = stretches[c]
-            g4 = sb("g4_%d" % c, [P, PACK, hi - lo], F32)
-            z2 = sb("z2_%d" % c, [P, PACK, hi - lo], F32)
+            g4 = sb("g4_%d" % c, [P, PACK, hi - lo], F32, "z_in" if c == 1 else None)
             for t in range(PACK):
                 nc.vector.tensor_copy(g4[:, t, :], yb[t][:].indirect(entries(l4, lo, hi)))
+            if c > 0:
+                s_columns(c - 1, z2_in[c - 1])
+            z2 = sb("z2_%d" % c, [P, PACK, hi - lo], F32, "z2in%d" % (c - 1) if c > 0 else None)
             for t in range(PACK):
                 nc.vector.tensor_tensor(z2[:, t, :], y[t][:].indirect(entries(l5, lo, hi)), g4[:, t, :], MULT)
             return z2
@@ -180,18 +187,16 @@ def tile_picked_selfdotprodhopmx_none_po_kernel(
             nc.scalar.activation(ya[t][:, cols], src, COPY, scale=-0.0625)
             nc.scalar.activation(v[t][:, cols], src, COPY, scale=-0.0625)
 
+        z2_in = []
         z2_0 = z2_lookups(0)
         nc.vector.quantize_mx(zq[:].bitcast(FP8X4), zs[:], z_in[:])
-        in_0 = interleave("z2in0", z2_0[:], nc.scalar.copy)
+        z2_in.append(interleave("z2in0", z2_0[:], nc.scalar.copy))
         z2_1 = z2_lookups(1)
-        s_columns(0, in_0)
-        in_1 = interleave("z2in1", z2_1[:], nc.scalar.copy)
+        z2_in.append(interleave("z2in1", z2_1[:], nc.scalar.copy))
         for t in range(PACK):
             s_out(t, 0)
         z2_2 = z2_lookups(2)
-        in_2 = interleave("z2in2", z2_2[:], nc.vector.tensor_copy)
-        s_columns(1, in_1)
-        s_columns(2, in_2)
+        s_columns(2, interleave("z2in2", z2_2[:], nc.vector.tensor_copy))
         for t in range(PACK):
             s_out(t, 1)
 

@@ -45,21 +45,25 @@ def tile_picked_selfdotprodhopmx_none_po_kernel(
             nc.sync.dma_start(tile[:], src)
             return tile
 
-        def load_scales(tile, src, queue):
+        def load_scales(tile, src):
             for q in range(4):
-                queue.dma_start(tile[32 * q : 32 * (q + 1), :].bitcast(I32), src[0, 4 * q : 4 * q + 4, :].bitcast(I32).partition_broadcast(8))
+                nc.sync.dma_start(tile[32 * q : 32 * q + 4, :].bitcast(I32), src[0, 4 * q : 4 * q + 4, :].bitcast(I32))
 
         xs = sb("xs", [P, T], U8)
         ws = sb("ws", [P, S], U8)
-        ga_t = sb("ga_t", [P, PACK], F32)
-        nc.scalar.dma_start(ga_t[:], ga.rearrange("(p t) o -> p (t o)", t=PACK))
-        load_scales(xs, x_scales, nc.sync)
+        nc.gpsimd.memset(xs[:].bitcast(I32), 0)
+        nc.gpsimd.memset(ws[:].bitcast(I32), 0)
         picks = load_list("picks", offs)
         xw = sb("xw", [P, T], I32)
-        nc.sync.dma_start(xw[:], x_words[0].rearrange("p n t -> p (n t)").bitcast(I32))
-        load_scales(ws, w1_scales, nc.sync)
+        x_src = x_words[0].rearrange("p n t -> p (n t)").bitcast(I32)
+        nc.sync.dma_start(xw[:, : T // 2], x_src[:, : T // 2])
+        load_scales(xs, x_scales)
+        nc.sync.dma_start(xw[:, T // 2 :], x_src[:, T // 2 :])
         ww = sb("ww", [P, S], I32)
         nc.sync.dma_start(ww[:], w1_words[0].rearrange("p n t -> p (n t)").bitcast(I32))
+        load_scales(ws, w1_scales)
+        ga_t = sb("ga_t", [P, PACK], F32)
+        nc.sync.dma_start(ga_t[:], ga.rearrange("(p t) o -> p (t o)", t=PACK))
         l2 = load_list("l2", n2)
         l1 = load_list("l1", n1)
         l3 = load_list("l3", n3)
@@ -73,24 +77,29 @@ def tile_picked_selfdotprodhopmx_none_po_kernel(
         ident = sb("ident", [P, P], F32)
         make_identity(nc, ident[:])
 
+        ca = sb("ca", [P, PACK], F32)
+        nc.scalar.activation(ca[:], ga_t[:], COPY, scale=0.75)
         y = [sb("y%d" % t, [P, WIDE], F32) for t in range(PACK)]
-        ya = [sb("ya%d" % t, [P, WIDE], F32) for t in range(PACK)]
+        ya = [sb("ya%d" % t, [P, S], F32) for t in range(PACK)]
         yb = [sb("yb%d" % t, [P, S], F32) for t in range(PACK)]
         for t in range(PACK):
-            engine = nc.vector if t < 2 else nc.gpsimd
-            engine.memset(ya[t][:, S:], 0.0)
-            engine.memset(y[t][:, S:], 0.0)
+            nc.vector.memset(y[t][:, S:], 0.0)
 
         xgs = sb("xgs", [P, S], U8)
         nc.vector.tensor_copy(xgs[:], xs[:].indirect(picks[:]))
-        wd = sb("wd", [P, S], I32)
-        wds = sb("wds", [P, S], U8)
-        wd_to = wd[:].rearrange("p (t m) -> p t m", t=PACK)
-        wd_from = ww[:].rearrange("p (m t) -> p t m", t=PACK)
-        wds_to = wds[:].rearrange("p (t m) -> p t m", t=PACK)
-        wds_from = ws[:].rearrange("p (m t) -> p t m", t=PACK)
         xg = sb("xg", [P, S], U32)
         half = S // 2
+        for lo in (0, half):
+            nc.vector.tensor_copy(xg[:, lo : lo + half], xw[:].bitcast(U32).indirect(entries(picks, lo, lo + half)))
+        ww_dealt = ww[:].rearrange("p (m t) -> p t m", t=PACK)
+        ws_dealt = ws[:].rearrange("p (m t) -> p t m", t=PACK)
+        wd0 = sb("wd0", [P, P], I32)
+        wds = sb("wds", [P, PACK, P], U8)
+        nc.vector.tensor_copy(wd0[:], ww_dealt[:, 0, :])
+        nc.vector.tensor_copy(wds[:, 0, :], ws_dealt[:, 0, :])
+        nc.vector.tensor_copy(wds[:, 1:, :], ws_dealt[:, 1:, :])
+        wd_rest = sb("wd_rest", [P, PACK - 1, P], I32, "ws")
+        nc.vector.tensor_copy(wd_rest[:], ww_dealt[:, 1:, :])
 
         def mx(out, codes_l, scales_l, codes_r, scales_r):
             nc.tensor.matmul_mx(out, lhsT=codes_l.bitcast(FP8X4), lhsT_scale=scales_l, rhs=codes_r.bitcast(FP8X4),
@@ -99,20 +108,13 @@ def tile_picked_selfdotprodhopmx_none_po_kernel(
         first_banks = [banks[0], banks[4]]
         for h in range(2):
             cols = slice(h * half, (h + 1) * half)
-            nc.vector.tensor_copy(xg[:, cols], xw[:].bitcast(U32).indirect(entries(picks, h * half, (h + 1) * half)))
-            if h == 0:
-                nc.vector.tensor_copy(wds_to[:, 0, :], wds_from[:, 0, :])
-                nc.vector.tensor_copy(wd_to[:, 0, :], wd_from[:, 0, :])
-            else:
-                nc.vector.tensor_copy(wds_to[:, 1:, :], wds_from[:, 1:, :])
-                nc.vector.tensor_copy(wd_to[:, 1:, :], wd_from[:, 1:, :])
-            mx(first_banks[h][:, :half], wd[:, :P], wds[:, :P], xg[:, cols], xgs[:, cols])
-            nc.scalar.activation(ya[0][:, cols], first_banks[h][:, :half], COPY, scale=ga_t[:, 0:1])
-            nc.scalar.copy(y[0][:, cols], first_banks[h][:, :half])
+            mx(first_banks[h][:, :half], wd0[:], wds[:, 0, :], xg[:, cols], xgs[:, cols])
+            nc.scalar.activation(ya[0][:, cols], first_banks[h][:, :half], COPY, scale=ca[:, 0:1])
+        for h in range(2):
+            nc.scalar.copy(y[0][:, h * half : (h + 1) * half], first_banks[h][:, :half])
         for t in range(1, PACK):
-            rows = slice(t * P, (t + 1) * P)
-            mx(banks[t][:], wd[:, rows], wds[:, rows], xg[:], xgs[:])
-            nc.scalar.activation(ya[t][:, :S], banks[t][:], COPY, scale=ga_t[:, t : t + 1])
+            mx(banks[t][:], wd_rest[:, t - 1, :], wds[:, t, :], xg[:], xgs[:])
+            nc.scalar.activation(ya[t][:], banks[t][:], COPY, scale=ca[:, t : t + 1])
             nc.scalar.copy(y[t][:, :S], banks[t][:])
         for h in range(2):
             cols = slice(h * half, (h + 1) * half)
@@ -124,7 +126,8 @@ def tile_picked_selfdotprodhopmx_none_po_kernel(
             g2 = sb("g2_%d" % t, [P, S], F32)
             prod1 = sb("prod1_%d" % t, [P, S], F32)
             prod23 = sb("prod23_%d" % t, [P, S], F32)
-            nc.vector.tensor_copy(g2[:], ya[t][:].indirect(l2[:]))
+            for lo in (0, half):
+                nc.vector.tensor_copy(g2[:, lo : lo + half], ya[t][:].indirect(entries(l2, lo, lo + half)))
             nc.vector.tensor_tensor(prod1[:], y[t][:].indirect(l1[:]), ya[t][:, :S], MULT)
             nc.vector.tensor_tensor(prod23[:], y[t][:].indirect(l3[:]), g2[:], MULT)
             for b in range(4):
@@ -138,8 +141,8 @@ def tile_picked_selfdotprodhopmx_none_po_kernel(
             for bb in range(2):
                 b = 2 * h + bb
                 zt = sb("zt%d" % b, [P, S], BF16)
-                nc.scalar.activation(zt[:].rearrange("q (u p e) -> q u p e", u=2, e=2),
-                                     banks[4 + b][:].rearrange("q (u e p) -> q u p e", u=2, e=2), COPY, scale=0.75)
+                nc.scalar.copy(zt[:].rearrange("q (u p e) -> q u p e", u=2, e=2),
+                               banks[4 + b][:].rearrange("q (u e p) -> q u p e", u=2, e=2))
                 for u in range(2):
                     nc.tensor.transpose(banks[h][:, u * half + bb * P : u * half + (bb + 1) * P],
                                         zt[:].bitcast(F32)[:, u * P : (u + 1) * P], ident[:])
@@ -150,14 +153,16 @@ def tile_picked_selfdotprodhopmx_none_po_kernel(
         v = [sb("v%d" % t, [P, S], F32) for t in range(PACK)]
         stretches = [(0, 256), (256, 384), (384, 512)]
 
-        def z2_lookups(c):
+        def z2_first(c, slot):
             lo, hi = stretches[c]
-            g4 = sb("g4_%d" % c, [P, PACK, hi - lo], F32, "z_in" if c == 1 else None)
+            g4 = sb("g4_%d" % c, [P, PACK, hi - lo], F32, slot)
             for t in range(PACK):
                 nc.vector.tensor_copy(g4[:, t, :], yb[t][:].indirect(entries(l4, lo, hi)))
-            if c > 0:
-                s_columns(c - 1, z2_in[c - 1])
-            z2 = sb("z2_%d" % c, [P, PACK, hi - lo], F32, "z2in%d" % (c - 1) if c > 0 else None)
+            return g4
+
+        def z2_second(c, g4, slot):
+            lo, hi = stretches[c]
+            z2 = sb("z2_%d" % c, [P, PACK, hi - lo], F32, slot)
             for t in range(PACK):
                 nc.vector.tensor_tensor(z2[:, t, :], y[t][:].indirect(entries(l5, lo, hi)), g4[:, t, :], MULT)
             return z2
@@ -168,6 +173,15 @@ def tile_picked_selfdotprodhopmx_none_po_kernel(
             copy(dst[:].rearrange("p (c t) -> p c t", t=PACK), src.rearrange("p t c -> p c t"))
             return dst
 
+        def s_place(t, lo, hi):
+            if t >= 2:
+                return banks[4 + t][:, lo:hi]
+            if lo < half:
+                return banks[2][:, t * half + lo : t * half + hi]
+            if t == 1:
+                return banks[5][:, lo:hi]
+            return banks[3 if lo < 384 else 4][:, lo:hi]
+
         def s_columns(c, z2_in):
             lo, hi = stretches[c]
             codes = sb("z2q%d" % c, [P, hi - lo], U32)
@@ -175,34 +189,34 @@ def tile_picked_selfdotprodhopmx_none_po_kernel(
             nc.vector.quantize_mx(codes[:].bitcast(FP8X4), scales[:], z2_in[:])
             for t in range(PACK):
                 rows = slice(t * P, (t + 1) * P)
-                if c == 0:
-                    dst = banks[2 + t // 2][:, (t % 2) * half : (t % 2 + 1) * half]
-                else:
-                    dst = banks[4 + t][:, lo - half : hi - half]
-                mx(dst, zq[:, rows], zs[:, rows], codes[:], scales[:])
+                mx(s_place(t, lo, hi), zq[:, rows], zs[:, rows], codes[:], scales[:])
 
-        def s_out(t, h):
-            cols = slice(h * half, (h + 1) * half)
-            src = banks[2 + t // 2][:, (t % 2) * half : (t % 2 + 1) * half] if h == 0 else banks[4 + t][:, :half]
-            nc.scalar.activation(ya[t][:, cols], src, COPY, scale=-0.0625)
-            nc.scalar.activation(v[t][:, cols], src, COPY, scale=-0.0625)
+        def s_out(t, lo, hi):
+            nc.scalar.activation(ya[t][:, lo:hi], s_place(t, lo, hi), COPY, scale=-0.0625)
+            nc.scalar.activation(v[t][:, lo:hi], s_place(t, lo, hi), COPY, scale=-0.0625)
 
-        z2_in = []
-        z2_0 = z2_lookups(0)
+        in_0 = interleave("z2in0", z2_second(0, z2_first(0, None), None)[:], nc.scalar.copy)
+        g4_1 = z2_first(1, None)
         nc.vector.quantize_mx(zq[:].bitcast(FP8X4), zs[:], z_in[:])
-        z2_in.append(interleave("z2in0", z2_0[:], nc.scalar.copy))
-        z2_1 = z2_lookups(1)
-        z2_in.append(interleave("z2in1", z2_1[:], nc.scalar.copy))
-        for t in range(PACK):
-            s_out(t, 0)
-        z2_2 = z2_lookups(2)
-        s_columns(2, interleave("z2in2", z2_2[:], nc.vector.tensor_copy))
-        for t in range(PACK):
-            s_out(t, 1)
+        in_1 = interleave("z2in1", z2_second(1, g4_1, "z_in")[:], nc.scalar.copy)
+        s_columns(0, in_0)
+        s_out(0, 0, half)
+        s_out(1, 0, half)
+        g4_2 = z2_first(2, "z2in0")
+        s_columns(1, in_1)
+        s_out(0, half, 384)
+        in_2 = interleave("z2in2", z2_second(2, g4_2, "z2in1")[:], nc.vector.tensor_copy)
+        s_columns(2, in_2)
+        s_out(0, 384, S)
+        s_out(1, half, S)
+        s_out(2, 0, S)
+        s_out(3, 0, S)
 
         st = [sb("st%d" % t, [P, S], F32) for t in range(PACK)]
         for t in range(PACK):
-            nc.vector.tensor_tensor(st[t][:], ya[t][:].indirect(l6[:]), v[t][:], SUB)
+            for lo in (0, half):
+                cols = slice(lo, lo + half)
+                nc.vector.tensor_tensor(st[t][:, cols], ya[t][:].indirect(entries(l6, lo, lo + half)), v[t][:, cols], SUB)
         out_rows = out_0.rearrange("(p t) j -> p t j", t=PACK)
         out_words = out_1[0].rearrange("p n t -> p (n t)").bitcast(I32)
         oq = sb("oq", [P, S], U32)

@@ -80,10 +80,11 @@ def tile_picked_selfdotprodhopmx_none_po_kernel(
         ca = sb("ca", [P, PACK], F32)
         nc.scalar.activation(ca[:], ga_t[:], COPY, scale=0.75)
         y = [sb("y%d" % t, [P, WIDE], F32) for t in range(PACK)]
-        ya = [sb("ya%d" % t, [P, S], F32) for t in range(PACK)]
+        ya = [sb("ya%d" % t, [P, WIDE], F32) for t in range(PACK)]
         yb = [sb("yb%d" % t, [P, S], F32) for t in range(PACK)]
         for t in range(PACK):
             nc.vector.memset(y[t][:, S:], 0.0)
+            nc.scalar.copy(ya[t][:, S:], y[t][:, S:])
 
         xgs = sb("xgs", [P, S], U8)
         nc.vector.tensor_copy(xgs[:], xs[:].indirect(picks[:]))
@@ -114,7 +115,7 @@ def tile_picked_selfdotprodhopmx_none_po_kernel(
             nc.scalar.copy(y[0][:, h * half : (h + 1) * half], first_banks[h][:, :half])
         for t in range(1, PACK):
             mx(banks[t][:], wd_rest[:, t - 1, :], wds[:, t, :], xg[:], xgs[:])
-            nc.scalar.activation(ya[t][:], banks[t][:], COPY, scale=ca[:, t : t + 1])
+            nc.scalar.activation(ya[t][:, :S], banks[t][:], COPY, scale=ca[:, t : t + 1])
             nc.scalar.copy(y[t][:, :S], banks[t][:])
         for h in range(2):
             cols = slice(h * half, (h + 1) * half)
@@ -126,8 +127,7 @@ def tile_picked_selfdotprodhopmx_none_po_kernel(
             g2 = sb("g2_%d" % t, [P, S], F32)
             prod1 = sb("prod1_%d" % t, [P, S], F32)
             prod23 = sb("prod23_%d" % t, [P, S], F32)
-            for lo in (0, half):
-                nc.vector.tensor_copy(g2[:, lo : lo + half], ya[t][:].indirect(entries(l2, lo, lo + half)))
+            nc.vector.tensor_copy(g2[:], ya[t][:].indirect(l2[:]))
             nc.vector.tensor_tensor(prod1[:], y[t][:].indirect(l1[:]), ya[t][:, :S], MULT)
             nc.vector.tensor_tensor(prod23[:], y[t][:].indirect(l3[:]), g2[:], MULT)
             for b in range(4):
@@ -136,7 +136,7 @@ def tile_picked_selfdotprodhopmx_none_po_kernel(
                 nc.tensor.matmul(dst, prod1[:, cols], ident[:], start=True, stop=False, is_transpose=True)
                 nc.tensor.matmul(dst, prod23[:, cols], ident[:], start=False, stop=True, is_transpose=True)
         z_in = sb("z_in", [P, PACK * S], BF16)
-        z_pairs = z_in[:].bitcast(F32).rearrange("p (t m u) -> p t m u", t=PACK, u=2)
+        z_pairs = z_in[:].bitcast(F32).rearrange("p (t m u) -> p m u t", t=PACK, u=2)
         for h in range(2):
             for bb in range(2):
                 b = 2 * h + bb
@@ -146,23 +146,20 @@ def tile_picked_selfdotprodhopmx_none_po_kernel(
                 for u in range(2):
                     nc.tensor.transpose(banks[h][:, u * half + bb * P : u * half + (bb + 1) * P],
                                         zt[:].bitcast(F32)[:, u * P : (u + 1) * P], ident[:])
-            nc.scalar.copy(z_pairs[:, :, 64 * h : 64 * (h + 1), :], banks[h][:].rearrange("p (u m t) -> p t m u", u=2, t=PACK))
-        zq = sb("zq", [P, S], U32)
+            nc.scalar.copy(z_pairs[:, 64 * h : 64 * (h + 1), :, :], banks[h][:].rearrange("p (u m t) -> p m u t", u=2, t=PACK))
         zs = sb("zs", [P, S], U8)
 
         v = [sb("v%d" % t, [P, S], F32) for t in range(PACK)]
-        stretches = [(0, 256), (256, 384), (384, 512)]
+        cut = 384
 
-        def z2_first(c, slot):
-            lo, hi = stretches[c]
-            g4 = sb("g4_%d" % c, [P, PACK, hi - lo], F32, slot)
+        def z2_first(lo, hi):
+            g4 = sb("g4_%d" % lo, [P, PACK, hi - lo], F32)
             for t in range(PACK):
                 nc.vector.tensor_copy(g4[:, t, :], yb[t][:].indirect(entries(l4, lo, hi)))
             return g4
 
-        def z2_second(c, g4, slot):
-            lo, hi = stretches[c]
-            z2 = sb("z2_%d" % c, [P, PACK, hi - lo], F32, slot)
+        def z2_second(lo, hi, g4, slot):
+            z2 = sb("z2_%d" % lo, [P, PACK, hi - lo], F32, slot)
             for t in range(PACK):
                 nc.vector.tensor_tensor(z2[:, t, :], y[t][:].indirect(entries(l5, lo, hi)), g4[:, t, :], MULT)
             return z2
@@ -170,22 +167,17 @@ def tile_picked_selfdotprodhopmx_none_po_kernel(
         def interleave(name, src, copy):
             width = src.shape[2]
             dst = sb(name, [P, PACK * width], BF16)
-            copy(dst[:].rearrange("p (c t) -> p c t", t=PACK), src.rearrange("p t c -> p c t"))
+            copy(dst[:].rearrange("p (c i t) -> p c t i", i=4, t=PACK), src.rearrange("p t (c i) -> p c t i", i=4))
             return dst
 
         def s_place(t, lo, hi):
             if t >= 2:
                 return banks[4 + t][:, lo:hi]
-            if lo < half:
-                return banks[2][:, t * half + lo : t * half + hi]
-            if t == 1:
-                return banks[5][:, lo:hi]
-            return banks[3 if lo < 384 else 4][:, lo:hi]
+            return banks[2 + t if lo < cut else 4 + t][:, lo:hi]
 
-        def s_columns(c, z2_in):
-            lo, hi = stretches[c]
-            codes = sb("z2q%d" % c, [P, hi - lo], U32)
-            scales = sb("z2s%d" % c, [P, hi - lo], U8)
+        def s_columns(lo, hi, z2_in):
+            codes = sb("z2q%d" % lo, [P, hi - lo], U32)
+            scales = sb("z2s%d" % lo, [P, hi - lo], U8)
             nc.vector.quantize_mx(codes[:].bitcast(FP8X4), scales[:], z2_in[:])
             for t in range(PACK):
                 rows = slice(t * P, (t + 1) * P)
@@ -195,28 +187,26 @@ def tile_picked_selfdotprodhopmx_none_po_kernel(
             nc.scalar.activation(ya[t][:, lo:hi], s_place(t, lo, hi), COPY, scale=-0.0625)
             nc.scalar.activation(v[t][:, lo:hi], s_place(t, lo, hi), COPY, scale=-0.0625)
 
-        in_0 = interleave("z2in0", z2_second(0, z2_first(0, None), None)[:], nc.scalar.copy)
-        g4_1 = z2_first(1, None)
+        z2_a = z2_second(0, cut, z2_first(0, cut), None)
+        in_0 = interleave("z2in0", z2_a[:, :, :half], nc.scalar.copy)
+        in_1 = interleave("z2in1", z2_a[:, :, half:], nc.scalar.copy)
+        g4_b = z2_first(cut, S)
+        zq = sb("zq", [P, S], U32, "yb3")
         nc.vector.quantize_mx(zq[:].bitcast(FP8X4), zs[:], z_in[:])
-        in_1 = interleave("z2in1", z2_second(1, g4_1, "z_in")[:], nc.scalar.copy)
-        s_columns(0, in_0)
-        s_out(0, 0, half)
-        s_out(1, 0, half)
-        g4_2 = z2_first(2, "z2in0")
-        s_columns(1, in_1)
-        s_out(0, half, 384)
-        in_2 = interleave("z2in2", z2_second(2, g4_2, "z2in1")[:], nc.vector.tensor_copy)
-        s_columns(2, in_2)
-        s_out(0, 384, S)
-        s_out(1, half, S)
+        s_columns(0, half, in_0)
+        s_columns(half, cut, in_1)
+        s_out(0, 0, cut)
+        s_out(1, 0, cut)
+        in_2 = interleave("z2in2", z2_second(cut, S, g4_b, "z2in0")[:], nc.vector.tensor_copy)
+        s_columns(cut, S, in_2)
+        s_out(0, cut, S)
+        s_out(1, cut, S)
         s_out(2, 0, S)
         s_out(3, 0, S)
 
         st = [sb("st%d" % t, [P, S], F32) for t in range(PACK)]
         for t in range(PACK):
-            for lo in (0, half):
-                cols = slice(lo, lo + half)
-                nc.vector.tensor_tensor(st[t][:, cols], ya[t][:].indirect(entries(l6, lo, lo + half)), v[t][:, cols], SUB)
+            nc.vector.tensor_tensor(st[t][:], ya[t][:].indirect(l6[:]), v[t][:], SUB)
         out_rows = out_0.rearrange("(p t) j -> p t j", t=PACK)
         out_words = out_1[0].rearrange("p n t -> p (n t)").bitcast(I32)
         oq = sb("oq", [P, S], U32)

from contextlib import ExitStack

import concourse.mybir as mybir
from concourse.masks import make_identity

F32 = mybir.dt.float32
BF16 = mybir.dt.bfloat16
I32 = mybir.dt.int32
U32 = mybir.dt.uint32
U16 = mybir.dt.uint16
U8 = mybir.dt.uint8
FP8X4 = mybir.dt.float8_e4m3fn_x4
MULT = mybir.AluOpType.mult
SUB = mybir.AluOpType.subtract
MAX = mybir.AluOpType.max
COPY = mybir.ActivationFunctionType.Copy

P = 128
PACK = 4
T = 2048
S = 512
WIDE = 2 * S
FLOPS = 2 * 2 * 512 * 512 * 512


def entries(offsets, lo, hi):
    return offsets[:, lo // 16 : hi // 16]


def tile_picked_selfdotprodhopmx_none_po_kernel(
    tc, x_words, x_scales, w1_words, w1_scales, ga, gb, offs, n1, n2, n3, n4, n5, n6, n7, out_0, out_1, out_2
):
    nc = tc.nc
    with ExitStack() as ctx:
        keep = ctx.enter_context(tc.tile_pool(name="keep", bufs=1))
        psum = ctx.enter_context(tc.psum_pool(name="psum", bufs=1))

        def sb(name, shape, dtype, tag=None):
            return keep.tile(shape, dtype, name=name, tag=tag or name, align_bytes=64)

        banks = [psum.tile([P, S], F32, name="bank%d" % b) for b in range(8)]

        def load_list(name, src):
            tile = keep.tile([P, S // 16], U16, name=name)
            nc.sync.dma_start(tile[:], src)
            return tile

        def load_scales(tile, src):
            for q in range(4):
                nc.sync.dma_start(tile[32 * q : 32 * q + 4, :].bitcast(I32), src[0, 4 * q : 4 * q + 4, :].bitcast(I32))

        xs = sb("xs", [P, T], U8)
        ws = sb("ws", [P, S], U8)
        nc.gpsimd.memset(xs[:].bitcast(I32), 0)
        nc.gpsimd.memset(ws[:].bitcast(I32), 0)
        picks = load_list("picks", offs)
        xw = sb("xw", [P, T], I32)
        x_src = x_words[0].rearrange("p n t -> p (n t)").bitcast(I32)
        nc.sync.dma_start(xw[:, : T // 2], x_src[:, : T // 2])
        load_scales(xs, x_scales)
        nc.sync.dma_start(xw[:, T // 2 :], x_src[:, T // 2 :])
        ww = sb("ww", [P, S], I32)
        nc.sync.dma_start(ww[:], w1_words[0].rearrange("p n t -> p (n t)").bitcast(I32))
        load_scales(ws, w1_scales)
        ga_t = sb("ga_t", [P, PACK], F32)
        nc.sync.dma_start(ga_t[:], ga.rearrange("(p t) o -> p (t o)", t=PACK))
        l2 = load_list("l2", n2)
        l1 = load_list("l1", n1)
        l3 = load_list("l3", n3)
        gb_t = sb("gb_t", [P, PACK], F32)
        nc.sync.dma_start(gb_t[:], gb.rearrange("(p t) o -> p (t o)", t=PACK))
        l4 = load_list("l4", n4)
        l5 = load_list("l5", n5)
        l6 = load_list("l6", n6)
        l7 = load_list("l7", n7)

        ident = sb("ident", [P, P], F32)
        make_identity(nc, ident[:])

        ca = sb("ca", [P, PACK], F32)
        nc.scalar.activation(ca[:], ga_t[:], COPY, scale=0.75)
        y = [sb("y%d" % t, [P, WIDE], F32) for t in range(PACK)]
        ya = [sb("ya%d" % t, [P, WIDE], F32) for t in range(PACK)]
        yb = [sb("yb%d" % t, [P, S], F32) for t in range(PACK)]
        for t in range(PACK):
            nc.vector.memset(y[t][:, S:], 0.0)
            nc.scalar.copy(ya[t][:, S:], y[t][:, S:])

        xgs = sb("xgs", [P, S], U8)
        nc.vector.tensor_copy(xgs[:], xs[:].indirect(picks[:]))
        xg = sb("xg", [P, S], U32)
        half = S // 2
        for lo in (0, half):
            nc.vector.tensor_copy(xg[:, lo : lo + half], xw[:].bitcast(U32).indirect(entries(picks, lo, lo + half)))
        ww_dealt = ww[:].rearrange("p (m t) -> p t m", t=PACK)
        ws_dealt = ws[:].rearrange("p (m t) -> p t m", t=PACK)
        wd0 = sb("wd0", [P, P], I32)
        wds = sb("wds", [P, PACK, P], U8)
        nc.vector.tensor_copy(wd0[:], ww_dealt[:, 0, :])
        nc.vector.tensor_copy(wds[:, 0, :], ws_dealt[:, 0, :])
        nc.vector.tensor_copy(wds[:, 1:, :], ws_dealt[:, 1:, :])
        wd_rest = sb("wd_rest", [P, PACK - 1, P], I32, "ws")
        nc.vector.tensor_copy(wd_rest[:], ww_dealt[:, 1:, :])

        def mx(out, codes_l, scales_l, codes_r, scales_r):
            nc.tensor.matmul_mx(out, lhsT=codes_l.bitcast(FP8X4), lhsT_scale=scales_l, rhs=codes_r.bitcast(FP8X4),
                                rhs_scale=scales_r, start=True, stop=True)

        first_banks = [banks[0], banks[4]]
        for h in range(2):
            cols = slice(h * half, (h + 1) * half)
            mx(first_banks[h][:, :half], wd0[:], wds[:, 0, :], xg[:, cols], xgs[:, cols])
            nc.scalar.activation(ya[0][:, cols], first_banks[h][:, :half], COPY, scale=ca[:, 0:1])
        for h in range(2):
            nc.scalar.copy(y[0][:, h * half : (h + 1) * half], first_banks[h][:, :half])
        for t in range(1, PACK):
            mx(banks[t][:], wd_rest[:, t - 1, :], wds[:, t, :], xg[:], xgs[:])
            nc.scalar.activation(ya[t][:, :S], banks[t][:], COPY, scale=ca[:, t : t + 1])
            nc.scalar.copy(y[t][:, :S], banks[t][:])
        for h in range(2):
            cols = slice(h * half, (h + 1) * half)
            nc.scalar.activation(yb[0][:, cols], first_banks[h][:, :half], COPY, scale=gb_t[:, 0:1])
        for t in range(1, PACK):
            nc.scalar.activation(yb[t][:], banks[t][:], COPY, scale=gb_t[:, t : t + 1])

        for t in range(PACK):
            g2 = sb("g2_%d" % t, [P, S], F32)
            prod1 = sb("prod1_%d" % t, [P, S], F32)
            prod23 = sb("prod23_%d" % t, [P, S], F32)
            nc.vector.tensor_copy(g2[:], ya[t][:].indirect(l2[:]))
            nc.vector.tensor_tensor(prod1[:], y[t][:].indirect(l1[:]), ya[t][:, :S], MULT)
            nc.vector.tensor_tensor(prod23[:], y[t][:].indirect(l3[:]), g2[:], MULT)
            for b in range(4):
                dst = banks[4 + b][:, t * P : (t + 1) * P]
                cols = slice(b * P, (b + 1) * P)
                nc.tensor.matmul(dst, prod1[:, cols], ident[:], start=True, stop=False, is_transpose=True)
                nc.tensor.matmul(dst, prod23[:, cols], ident[:], start=False, stop=True, is_transpose=True)
        z_in = sb("z_in", [P, PACK * S], BF16)
        z_pairs = z_in[:].bitcast(F32).rearrange("p (t m u) -> p m u t", t=PACK, u=2)
        for h in range(2):
            for bb in range(2):
                b = 2 * h + bb
                zt = sb("zt%d" % b, [P, S], BF16)
                nc.scalar.copy(zt[:].rearrange("q (u p e) -> q u p e", u=2, e=2),
                               banks[4 + b][:].rearrange("q (u e p) -> q u p e", u=2, e=2))
                for u in range(2):
                    nc.tensor.transpose(banks[h][:, u * half + bb * P : u * half + (bb + 1) * P],
                                        zt[:].bitcast(F32)[:, u * P : (u + 1) * P], ident[:])
            nc.scalar.copy(z_pairs[:, 64 * h : 64 * (h + 1), :, :], banks[h][:].rearrange("p (u m t) -> p m u t", u=2, t=PACK))
        zs = sb("zs", [P, S], U8)

        v = [sb("v%d" % t, [P, S], F32) for t in range(PACK)]
        cut = 384

        def z2_first(lo, hi):
            g4 = sb("g4_%d" % lo, [P, PACK, hi - lo], F32)
            for t in range(PACK):
                nc.vector.tensor_copy(g4[:, t, :], yb[t][:].indirect(entries(l4, lo, hi)))
            return g4

        def z2_second(lo, hi, g4, slot):
            z2 = sb("z2_%d" % lo, [P, PACK, hi - lo], F32, slot)
            for t in range(PACK):
                nc.vector.tensor_tensor(z2[:, t, :], y[t][:].indirect(entries(l5, lo, hi)), g4[:, t, :], MULT)
            return z2

        def interleave(name, src, copy):
            width = src.shape[2]
            dst = sb(name, [P, PACK * width], BF16)
            copy(dst[:].rearrange("p (c i t) -> p c t i", i=4, t=PACK), src.rearrange("p t (c i) -> p c t i", i=4))
            return dst

        def s_place(t, lo, hi):
            if t >= 2:
                return banks[4 + t][:, lo:hi]
            return banks[2 + t if lo < cut else 4 + t][:, lo:hi]

        def s_columns(lo, hi, z2_in):
            codes = sb("z2q%d" % lo, [P, hi - lo], U32)
            scales = sb("z2s%d" % lo, [P, hi - lo], U8)
            nc.vector.quantize_mx(codes[:].bitcast(FP8X4), scales[:], z2_in[:])
            for t in range(PACK):
                rows = slice(t * P, (t + 1) * P)
                mx(s_place(t, lo, hi), zq[:, rows], zs[:, rows], codes[:], scales[:])

        def s_out(t, lo, hi):
            nc.scalar.activation(ya[t][:, lo:hi], s_place(t, lo, hi), COPY, scale=-0.0625)
            nc.scalar.activation(v[t][:, lo:hi], s_place(t, lo, hi), COPY, scale=-0.0625)

        z2_a = z2_second(0, cut, z2_first(0, cut), None)
        in_0 = interleave("z2in0", z2_a[:, :, :half], nc.scalar.copy)
        in_1 = interleave("z2in1", z2_a[:, :, half:], nc.scalar.copy)
        g4_b = z2_first(cut, S)
        zq = sb("zq", [P, S], U32, "yb3")
        nc.vector.quantize_mx(zq[:].bitcast(FP8X4), zs[:], z_in[:])
        s_columns(0, half, in_0)
        s_columns(half, cut, in_1)
        s_out(0, 0, cut)
        s_out(1, 0, cut)
        in_2 = interleave("z2in2", z2_second(cut, S, g4_b, "z2in0")[:], nc.vector.tensor_copy)
        s_columns(cut, S, in_2)
        s_out(0, cut, S)
        s_out(1, cut, S)
        s_out(2, 0, S)
        s_out(3, 0, S)

        st = [sb("st%d" % t, [P, S], F32) for t in range(PACK)]
        for t in range(PACK):
            nc.vector.tensor_tensor(st[t][:], ya[t][:].indirect(l6[:]), v[t][:], SUB)
        out_rows = out_0.rearrange("(p t) j -> p t j", t=PACK)
        out_words = out_1[0].rearrange("p n t -> p (n t)").bitcast(I32)
        oq = sb("oq", [P, S], U32)
        osc = sb("osc", [P, S], U8)

        def out_lookups(name, lo, hi):
            g7 = sb("g7_" + name, [P, PACK, hi - lo], F32)
            res = sb("res_" + name, [P, PACK, hi - lo], F32)
            for t in range(PACK):
                nc.vector.tensor_copy(g7[:, t, :], st[t][:].indirect(entries(l7, lo, hi)))
            for t in range(PACK):
                nc.vector.tensor_tensor(res[:, t, :], g7[:, t, :], st[t][:, lo:hi], MAX)
            nc.sync.dma_start(out_rows[:, :, lo:hi], res[:])
            return res

        def out_planes(lo, hi, rounded):
            nc.vector.quantize_mx(oq[:, lo:hi].bitcast(FP8X4), osc[:, lo:hi], rounded[:])
            nc.sync.dma_start(out_words[:, lo:hi], oq[:, lo:hi].bitcast(I32))

        res_a = out_lookups("a", 0, 384)
        r0 = interleave("r0", res_a[:, :, 0:256], nc.scalar.copy)
        r1 = interleave("r1", res_a[:, :, 256:384], nc.scalar.copy)
        res_b = out_lookups("b", 384, 512)
        out_planes(0, 256, r0)
        r2 = interleave("r2", res_b[:], nc.vector.tensor_copy)
        out_planes(256, 384, r1)
        out_planes(384, 512, r2)
        for q in range(4):
            queue = nc.scalar if q % 2 == 0 else nc.sync
            queue.dma_start(out_2[0, 4 * q : 4 * q + 4, :].bitcast(I32), osc[32 * q : 32 * q + 4, :].bitcast(I32))
